import numpy as np, ml_dtypes
CORES = [29,45,93,109,157,173,221,237,285,301,349,365,413,429,477,493]
N = 16
TK = 256
WID = [32,256,160,256,192,128,160,224,192,160,32,256,256,160,64,192]
def setup_inputs(rng):
    rt = (0.75 * rng.standard_normal((128, 1), dtype=np.float32) + rng.standard_normal((128, N), dtype=np.float32) / 2).astype(ml_dtypes.bfloat16)
    return {"x": rng.standard_normal((N, 128, TK), dtype=np.float32).astype(ml_dtypes.bfloat16), "rt": np.broadcast_to(rt, (N, 128, N)).copy(), "w": rng.standard_normal((N, 128, 128), dtype=np.float32).astype(ml_dtypes.bfloat16)}
def setup_inputs_big(rng):
    d = setup_inputs(rng)
    for k in ("x", "w"): d[k] = (d[k].astype(np.float32) * 1024.0).astype(d[k].dtype)
    return d
def setup_inputs_small(rng):
    d = setup_inputs(rng)
    for k in ("x", "w"): d[k] = (d[k].astype(np.float32) * (1 / 1024.0)).astype(d[k].dtype)
    return d
def whole(x, rt, w):
    X, RT, W = x.astype(np.float64), rt.astype(np.float64), w.astype(np.float64)
    y = np.zeros((N, 128, TK))
    for r in range(N):
        sc = RT[r].T @ X[r]
        g = np.exp(sc - sc.max(axis=0)); g = g / g.sum(axis=0)
        y[r] = sum(g[j] * (W[j].T @ X[r]) for j in range(N))
    return {"y": y.astype(ml_dtypes.bfloat16)}
def reference(x, rt, w):
    o = whole(x, rt, w)["y"].copy()
    for r in range(N):
        o[r][:, WID[r]:] = np.nan
    return {"y": o}

@@ -1,0 +1,221 @@
+from concourse.bass import DstId, RemoteDMATransfer
+from concourse.mybir import AluOpType, AxisListType, ActivationFunctionType
+
+NE = 8
+TK = 256
+SCRATCH = {
+    "xo": ("sbuf", [128, TK], "bfloat16"),
+    "xp": ("sbuf", [128, TK], "bfloat16"),
+    "rts": ("sbuf", [128, 16], "bfloat16"),
+    "wall": ("sbuf", [128, NE * 128], "bfloat16"),
+    "ramp": ("sbuf", [128, 128], "bfloat16"),
+    "ident": ("sbuf", [128, 128], "bfloat16"),
+    "ones": ("sbuf", [128, 128], "bfloat16"),
+    "sel": ("sbuf", [128, NE * 128], "bfloat16"),
+    "nmx": ("sbuf", [128, 4], "float32"),
+    "zs": ("sbuf", [128, 4], "float32"),
+    "rz": ("sbuf", [128, 4], "float32"),
+    "ex": ("sbuf", [128, 64], "float32"),
+    "gm": ("sbuf", [128, 4 * NE], "bfloat16"),
+    "gts": ("sbuf", [128, 2 * TK], "bfloat16"),
+    "xg": ("sbuf", [128, 2 * NE * TK], "bfloat16"),
+    "pout": ("sbuf", [128, TK], "bfloat16"),
+    "pin": ("sbuf", [128, TK], "bfloat16"),
+    "yo": ("sbuf", [128, TK], "bfloat16"),
+    "sm0": ("psum", [128, 512], "float32"),
+    "sm1": ("psum", [128, 512], "float32"),
+    "acc0": ("psum", [128, 512], "float32"),
+    "acc1": ("psum", [128, 512], "float32"),
+    "gb0": ("psum", [128, 512], "float32"),
+    "gb1": ("psum", [128, 512], "float32"),
+    "gb2": ("psum", [128, 512], "float32"),
+    "gb3": ("psum", [128, 512], "float32"),
+}
+SEMAPHORES = ["xl", "rl", "wl", "st", "gi", "pe", "ve", "ac", "sent", "mp", "pa"] + ["w%d" % i for i in range(NE)]
+
+
+def _bits(m):
+    return bin(m).count("1")
+
+
+def rank_program(g, core, T, topo):
+    rank = T.rank_of(core)
+    if rank is None:
+        return
+    cores, wid = T.cores, T.tables["WID"]
+    N = len(cores)
+    rackl = sorted([rank] + [q for q in range(N) if q != rank and topo.same_plane(core, cores[q])])
+    idx = rackl.index(rank)
+    partner = [q for q in range(N) if topo.rack(topo.host(cores[q])) != topo.rack(topo.host(core))
+               and topo.may_write(core, cores[q]) and topo.chip(cores[q]) == topo.chip(core)][0]
+    pc = cores[partner]
+    nset = [wid[rank], wid[partner]]
+    xbuf = [T.xo, T.xp]
+    sm = [T.sm0, T.sm1]
+    acc = [T.acc0, T.acc1]
+    gb = [T.gb0, T.gb1, T.gb2, T.gb3]
+    S = T.sem
+    Q = {"pe": g.tensor, "ve": g.vector, "ac": g.scalar, "g": g, "sy": g.sync}
+    cnt = {"pe": 0, "ve": 0, "ac": 0}
+    seen = {}
+
+    def need(q, deps):
+        for sem, val in deps:
+            if seen.get((q, sem), 0) < val:
+                Q[q].wait_ge(S[sem], val)
+                seen[(q, sem)] = val
+
+    def done(q, ins):
+        ins.then_inc(S[q], 1)
+        cnt[q] += 1
+        return (q, cnt[q])
+
+    n0 = nset[0]
+    g.sync.dma_start(T.xo[:, 0:n0], T.x[:, 0:n0]).then_inc(S.xl, 16)
+    g.scalar.dma_start(T.wall[:, idx * 128:(idx + 1) * 128], T.w[:, :]).then_inc(S.wl, 16)
+    g.sync.dma_start(T.rts[:, :], T.rt[:, :]).then_inc(S.rl, 16)
+    XL, RL, WL = ("xl", 16), ("rl", 16), ("wl", 16)
+
+    g.iota(T.ramp[:, :], [[1, 128]], 0, -1, allow_small_or_imprecise_dtypes=True).then_inc(S.gi, 1)
+    d_ones = done("ve", g.vector.memset(T.ones[0:NE, :], 1.0))
+    d_zs = done("ve", g.vector.memset(T.zs[:, :], 1.0))
+    need("ve", [("gi", 1)])
+    d_id = done("ve", g.vector.tensor_scalar(T.ident[:, :], T.ramp[:, :], 0.0, None, AluOpType.is_equal))
+    need("ve", [d_id, d_ones])
+    d_sel = None
+    for j in range(NE):
+        d_sel = done("ve", g.vector.tensor_scalar(T.sel[0:NE, j * 128:(j + 1) * 128], T.ones[0:NE, :],
+                                                  T.ident[0:NE, j:j + 1], None, AluOpType.mult))
+
+    mx = topo.mask(core, pc)
+    rid, pid = topo.addr(pc, core)
+    need("g", [XL])
+    g.remote_dma(T.xp[:, 0:n0], T.xo[:, 0:n0], S.mp, S.sent, pid, rid, mx)
+    sent = _bits(mx)
+    order = [(idx - k) % NE for k in range(NE)]
+    dsts = [cores[rackl[(idx + k) % NE]] for k in range(1, NE)]
+    mw = topo.mask(core, dsts[0])
+    for d in dsts:
+        mw &= topo.mask(core, d)
+    slot = T.wall[:, idx * 128:(idx + 1) * 128]
+    ids = []
+    for d in dsts:
+        r_, p_ = topo.addr(d, core)
+        ids.append(DstId(rid=r_, pnc=p_))
+    need("g", [WL])
+    g.remote_dma_fused([RemoteDMATransfer(dst_ids=ids, dma_engine_mask=mw, remote_sem=S["w%d" % idx],
+                                          srcs=[slot], dsts=[slot for _ in dsts])], local_sem=S.sent)
+    sent += _bits(mw)
+    MP = ("mp", _bits(topo.mask(pc, core)))
+    arrive = [XL, MP]
+
+    def wdep(j):
+        if j == idx:
+            return WL
+        return ("w%d" % j, _bits(topo.mask(cores[rackl[j]], core)))
+
+    def blocks(n):
+        return [(b, min(128, n - 128 * b)) for b in range((n + 127) // 128)]
+
+    runs = []
+    for p, e in enumerate(rackl):
+        if runs and runs[-1][1] + runs[-1][2] == e:
+            runs[-1][2] += 1
+        else:
+            runs.append([p, e, 1])
+
+    def scores(s):
+        need("pe", [arrive[s], RL])
+        d = None
+        for b, nb in blocks(nset[s]):
+            d = done("pe", g.tensor.matmul(sm[s][0:nb, 16 * b:16 * b + 16], xbuf[s][:, 128 * b:128 * b + nb],
+                                           T.rts[:, :], True, True))
+        return d
+
+    def softmax(s, d_sc):
+        n = nset[s]
+        bl = blocks(n)
+        need("ve", [d_sc])
+        d = None
+        for b, nb in bl:
+            c = 2 * s + b
+            d = done("ve", g.vector.tensor_reduce(T.nmx[0:nb, c:c + 1], sm[s][0:nb, 16 * b:16 * b + 16],
+                                                  AxisListType.X, AluOpType.max, negate=True))
+        need("ac", [d, d_zs])
+        for b, nb in bl:
+            c = 2 * s + b
+            d = done("ac", g.scalar.activation(T.ex[0:nb, 16 * c:16 * c + 16], sm[s][0:nb, 16 * b:16 * b + 16],
+                                               ActivationFunctionType.Exp, bias=T.nmx[0:nb, c:c + 1], scale=1.0,
+                                               accum_out=T.zs[0:nb, c:c + 1]))
+        need("ve", [d])
+        d = done("ve", g.vector.reciprocal(T.rz[:, 2 * s:2 * s + len(bl)], T.zs[:, 2 * s:2 * s + len(bl)]))
+        need("ve", [d])
+        for b, nb in bl:
+            c = 2 * s + b
+            for p, e, l in runs:
+                d = done("ve", g.vector.tensor_scalar(T.gm[0:nb, NE * c + p:NE * c + p + l],
+                                                      T.ex[0:nb, 16 * c + e:16 * c + e + l],
+                                                      T.rz[0:nb, c:c + 1], None, AluOpType.mult))
+        return d
+
+    def turn(s, d_g):
+        n = nset[s]
+        need("pe", [d_g, d_id])
+        d = None
+        for b, nb in blocks(n):
+            c = 2 * s + b
+            d = done("pe", g.tensor.matmul(sm[s][0:NE, 128 + 128 * b:128 + 128 * b + nb], T.gm[0:nb, NE * c:NE * c + NE],
+                                           T.ident[0:nb, 0:nb], True, True))
+        need("ac", [d])
+        return done("ac", g.scalar.activation(T.gts[0:NE, TK * s:TK * s + n], sm[s][0:NE, 128:128 + n],
+                                              ActivationFunctionType.Copy))
+
+    ring = {"n": 0, "free": [None, None, None, None]}
+    xgd = {}
+
+    def gate(s, d_gt):
+        n = nset[s]
+        for j in order:
+            k = ring["n"] % 4
+            ring["n"] += 1
+            deps = [d_gt, d_sel]
+            if ring["free"][k] is not None:
+                deps.append(ring["free"][k])
+            need("pe", deps)
+            d = done("pe", g.tensor.matmul(gb[k][:, 0:n], T.sel[0:NE, j * 128:(j + 1) * 128],
+                                           T.gts[0:NE, TK * s:TK * s + n], True, True))
+            need("ve", [d, arrive[s]])
+            o = (s * NE + j) * TK
+            d = done("ve", g.vector.tensor_tensor(T.xg[:, o:o + n], xbuf[s][:, 0:n], gb[k][:, 0:n], AluOpType.mult))
+            ring["free"][k] = d
+            xgd[(s, j)] = d
+
+    def main(s, js):
+        n = nset[s]
+        d = None
+        for j in js:
+            need("pe", [wdep(j), xgd[(s, j)]])
+            o = (s * NE + j) * TK
+            d = done("pe", g.tensor.matmul(acc[s][:, 0:n], T.wall[:, j * 128:(j + 1) * 128], T.xg[:, o:o + n],
+                                           j == order[0], j == order[-1]))
+        return d
+
+    gate(0, turn(0, softmax(0, scores(0))))
+    d_sc = scores(1)
+    main(0, order[0:1])
+    gate(1, turn(1, softmax(1, d_sc)))
+    d_p = main(1, order)
+    d_o = main(0, order[1:])
+    n1 = nset[1]
+    need("ac", [d_p])
+    d_ev = done("ac", g.scalar.activation(T.pout[:, 0:n1], acc[1][:, 0:n1], ActivationFunctionType.Copy))
+    need("g", [d_ev])
+    g.remote_dma(T.pin[:, 0:n1], T.pout[:, 0:n1], S.pa, S.sent, pid, rid, mx)
+    sent += _bits(mx)
+
+    need("ve", [d_o, ("pa", _bits(topo.mask(pc, core)))])
+    d_y = done("ve", g.vector.tensor_tensor(T.yo[:, 0:n0], T.pin[:, 0:n0], acc[0][:, 0:n0], AluOpType.add))
+    need("sy", [d_y])
+    g.sync.dma_start(T.y[:, 0:n0], T.yo[:, 0:n0]).then_inc(S.st, 16)
+    g.sync.wait_ge(S.st, 16)
+    g.wait_ge(S.sent, sent)

@@ -1,59 +1,129 @@
 from concourse.bass import DstId, RemoteDMATransfer
 from concourse.mybir import AluOpType, AxisListType, ActivationFunctionType
 
-NE = 8
+WORLD = 512
 TK = 256
+NX = 16
 SCRATCH = {
     "xo": ("sbuf", [128, TK], "bfloat16"),
     "xp": ("sbuf", [128, TK], "bfloat16"),
-    "rts": ("sbuf", [128, 16], "bfloat16"),
-    "wall": ("sbuf", [128, NE * 128], "bfloat16"),
+    "rts": ("sbuf", [128, NX], "bfloat16"),
+    "wall": ("sbuf", [128, NX * 128], "bfloat16"),
     "ramp": ("sbuf", [128, 128], "bfloat16"),
     "ident": ("sbuf", [128, 128], "bfloat16"),
-    "ones": ("sbuf", [128, 128], "bfloat16"),
-    "sel": ("sbuf", [128, NE * 128], "bfloat16"),
     "nmx": ("sbuf", [128, 4], "float32"),
     "zs": ("sbuf", [128, 4], "float32"),
     "rz": ("sbuf", [128, 4], "float32"),
-    "ex": ("sbuf", [128, 64], "float32"),
-    "gm": ("sbuf", [128, 4 * NE], "bfloat16"),
-    "gts": ("sbuf", [128, 2 * TK], "bfloat16"),
-    "xg": ("sbuf", [128, 2 * NE * TK], "bfloat16"),
+    "ex": ("sbuf", [128, 4 * NX], "float32"),
+    "dg": ("sbuf", [128, 4 * 128], "bfloat16"),
+    "zg": ("sbuf", [128, 4 * NX * 128], "bfloat16"),
     "pout": ("sbuf", [128, TK], "bfloat16"),
     "pin": ("sbuf", [128, TK], "bfloat16"),
     "yo": ("sbuf", [128, TK], "bfloat16"),
     "sm0": ("psum", [128, 512], "float32"),
-    "sm1": ("psum", [128, 512], "float32"),
-    "acc0": ("psum", [128, 512], "float32"),
-    "acc1": ("psum", [128, 512], "float32"),
-    "gb0": ("psum", [128, 512], "float32"),
-    "gb1": ("psum", [128, 512], "float32"),
-    "gb2": ("psum", [128, 512], "float32"),
-    "gb3": ("psum", [128, 512], "float32"),
+    "ap0": ("psum", [128, 512], "float32"),
+    "ap1": ("psum", [128, 512], "float32"),
+    "ao0": ("psum", [128, 512], "float32"),
+    "ao1": ("psum", [128, 512], "float32"),
+    "zp0": ("psum", [128, 512], "float32"),
+    "zp1": ("psum", [128, 512], "float32"),
+    "zp2": ("psum", [128, 512], "float32"),
 }
-SEMAPHORES = ["xl", "rl", "wl", "st", "gi", "pe", "ve", "ac", "sent", "mp", "pa"] + ["w%d" % i for i in range(NE)]
+SEMAPHORES = ["xl", "rl", "wl", "st", "gi", "pe", "ve", "ac", "sent", "mp", "pa", "cst", "hw"] + ["w%d" % i for i in range(NX)]
+
+_HC = {}
 
 
 def _bits(m):
     return bin(m).count("1")
 
 
+def _helper(topo, c):
+    if c not in _HC:
+        _HC[c] = [d for d in range(WORLD) if topo.host(d) == topo.host(c) and topo.chip(d) == topo.chip(c)
+                  and topo.die(d) != topo.die(c)][0]
+    return _HC[c]
+
+
+def _plan(topo, cores, q):
+    c = cores[q]
+    R = range(len(cores))
+    hl = [p for p in R if topo.host(cores[p]) == topo.host(c)]
+    ml = [p for p in R if topo.host(cores[p]) != topo.host(c) and topo.same_plane(c, cores[p])]
+    pa = [p for p in R if topo.rack(topo.host(cores[p])) != topo.rack(topo.host(c)) and topo.may_write(c, cores[p])
+          and topo.chip(cores[p]) == topo.chip(c)][0]
+    return hl, ml, pa, hl.index(q)
+
+
+def _crit(topo, cores, q):
+    hl, ml, pa, j = _plan(topo, cores, q)
+    H = len(hl)
+    return [ml[(j + k) % H] for k in range(H)] + [hl[(j + 1) % H]]
+
+
+def _late(topo, cores, q):
+    hl, ml, pa, j = _plan(topo, cores, q)
+    H = len(hl)
+    return [hl[(j + 2) % H], hl[(j + 3) % H], _plan(topo, cores, hl[(j - 1) % H])[2], _plan(topo, cores, hl[(j - 2) % H])[2]]
+
+
+def _mask(topo, src, dsts):
+    m = topo.mask(src, dsts[0])
+    for d in dsts:
+        m &= topo.mask(src, d)
+    return m
+
+
+def _chip_only(topo, src, on_chip, off_chip):
+    return topo.mask(src, on_chip) & ~topo.mask(src, off_chip)
+
+
+def _fan(g, T, topo, src, q, dsts, mask):
+    slot = T.wall[:, q * 128:(q + 1) * 128]
+    ids = []
+    for d in dsts:
+        r_, p_ = topo.addr(d, src)
+        ids.append(DstId(rid=r_, pnc=p_))
+    g.remote_dma_fused([RemoteDMATransfer(dst_ids=ids, dma_engine_mask=mask, remote_sem=T.sem["w%d" % q],
+                                          srcs=[slot], dsts=[slot for _ in dsts])], local_sem=T.sem.sent)
+
+
+def _helper_program(g, core, T, topo, q):
+    cores = T.cores
+    S = T.sem
+    rc = cores[q]
+    dsts = [cores[p] for p in _late(topo, cores, q)]
+    mh = _mask(topo, core, dsts)
+    g.iota(T.ramp[:, :], [[1, 128]], 0, -1, allow_small_or_imprecise_dtypes=True).then_inc(S.gi, 1)
+    g.vector.wait_ge(S.gi, 1)
+    g.vector.tensor_scalar(T.ident[:, :], T.ramp[:, :], 0.0, None, AluOpType.is_equal).then_inc(S.ve, 1)
+    g.wait_ge(S.ve, 1)
+    rid, pid = topo.addr(rc, core)
+    g.remote_dma(T.ident[:, :], T.ident[:, :], S.cst, S.sent, pid, rid, mh)
+    g.wait_ge(S.hw, _bits(_chip_only(topo, rc, core, dsts[0])))
+    _fan(g, T, topo, core, q, dsts, mh)
+    g.wait_ge(S.sent, 2 * _bits(mh))
+
+
 def rank_program(g, core, T, topo):
+    cores, wid = T.cores, T.tables["WID"]
     rank = T.rank_of(core)
     if rank is None:
+        for q in range(len(cores)):
+            if topo.host(cores[q]) == topo.host(core) and topo.chip(cores[q]) == topo.chip(core) \
+                    and _helper(topo, cores[q]) == core:
+                _helper_program(g, core, T, topo, q)
         return
-    cores, wid = T.cores, T.tables["WID"]
-    N = len(cores)
-    rackl = sorted([rank] + [q for q in range(N) if q != rank and topo.same_plane(core, cores[q])])
-    idx = rackl.index(rank)
-    partner = [q for q in range(N) if topo.rack(topo.host(cores[q])) != topo.rack(topo.host(core))
-               and topo.may_write(core, cores[q]) and topo.chip(cores[q]) == topo.chip(core)][0]
+    hl, ml, partner, i = _plan(topo, cores, rank)
+    H = len(hl)
+    phl, pml, _x, pi = _plan(topo, cores, partner)
     pc = cores[partner]
+    hc = _helper(topo, core)
+    EP = [rank] + [ml[(i - k) % H] for k in range(H)] + [hl[(i - 1) % H]]
+    EO = EP + [hl[(i - 2) % H], hl[(i - 3) % H], phl[(pi + 1) % H], phl[(pi + 2) % H]]
     nset = [wid[rank], wid[partner]]
     xbuf = [T.xo, T.xp]
-    sm = [T.sm0, T.sm1]
-    acc = [T.acc0, T.acc1]
-    gb = [T.gb0, T.gb1, T.gb2, T.gb3]
+    zp = [T.zp0, T.zp1, T.zp2]
     S = T.sem
     Q = {"pe": g.tensor, "ve": g.vector, "ac": g.scalar, "g": g, "sy": g.sync}
     cnt = {"pe": 0, "ve": 0, "ac": 0}
@@ -70,151 +140,149 @@ def rank_program(g, core, T, topo):
         cnt[q] += 1
         return (q, cnt[q])
 
-    n0 = nset[0]
+    n0, n1 = nset
+    own = T.wall[:, rank * 128:(rank + 1) * 128]
     g.sync.dma_start(T.xo[:, 0:n0], T.x[:, 0:n0]).then_inc(S.xl, 16)
-    g.scalar.dma_start(T.wall[:, idx * 128:(idx + 1) * 128], T.w[:, :]).then_inc(S.wl, 16)
+    g.scalar.dma_start(own, T.w[:, :]).then_inc(S.wl, 16)
     g.sync.dma_start(T.rts[:, :], T.rt[:, :]).then_inc(S.rl, 16)
     XL, RL, WL = ("xl", 16), ("rl", 16), ("wl", 16)
-
-    g.iota(T.ramp[:, :], [[1, 128]], 0, -1, allow_small_or_imprecise_dtypes=True).then_inc(S.gi, 1)
-    d_ones = done("ve", g.vector.memset(T.ones[0:NE, :], 1.0))
     d_zs = done("ve", g.vector.memset(T.zs[:, :], 1.0))
-    need("ve", [("gi", 1)])
-    d_id = done("ve", g.vector.tensor_scalar(T.ident[:, :], T.ramp[:, :], 0.0, None, AluOpType.is_equal))
-    need("ve", [d_id, d_ones])
-    d_sel = None
-    for j in range(NE):
-        d_sel = done("ve", g.vector.tensor_scalar(T.sel[0:NE, j * 128:(j + 1) * 128], T.ones[0:NE, :],
-                                                  T.ident[0:NE, j:j + 1], None, AluOpType.mult))
 
     mx = topo.mask(core, pc)
     rid, pid = topo.addr(pc, core)
     need("g", [XL])
     g.remote_dma(T.xp[:, 0:n0], T.xo[:, 0:n0], S.mp, S.sent, pid, rid, mx)
     sent = _bits(mx)
-    order = [(idx - k) % NE for k in range(NE)]
-    dsts = [cores[rackl[(idx + k) % NE]] for k in range(1, NE)]
-    mw = topo.mask(core, dsts[0])
-    for d in dsts:
-        mw &= topo.mask(core, d)
-    slot = T.wall[:, idx * 128:(idx + 1) * 128]
-    ids = []
-    for d in dsts:
-        r_, p_ = topo.addr(d, core)
-        ids.append(DstId(rid=r_, pnc=p_))
+    cd = [cores[p] for p in _crit(topo, cores, rank)]
+    mw = _mask(topo, core, cd)
     need("g", [WL])
-    g.remote_dma_fused([RemoteDMATransfer(dst_ids=ids, dma_engine_mask=mw, remote_sem=S["w%d" % idx],
-                                          srcs=[slot], dsts=[slot for _ in dsts])], local_sem=S.sent)
+    _fan(g, T, topo, core, rank, cd, mw)
     sent += _bits(mw)
+    ld = [cores[p] for p in _late(topo, cores, rank)]
+    mon = _chip_only(topo, core, hc, ld[0])
+    hr, hp = topo.addr(hc, core)
+    g.remote_dma(own, own, S.hw, S.sent, hp, hr, mon)
+    sent += _bits(mon)
     MP = ("mp", _bits(topo.mask(pc, core)))
     arrive = [XL, MP]
+    CST = ("cst", _bits(_mask(topo, hc, ld)))
 
     def wdep(j):
-        if j == idx:
+        if j == rank:
             return WL
-        return ("w%d" % j, _bits(topo.mask(cores[rackl[j]], core)))
+        if rank in _crit(topo, cores, j):
+            return ("w%d" % j, _bits(_mask(topo, cores[j], [cores[p] for p in _crit(topo, cores, j)])))
+        return ("w%d" % j, _bits(_mask(topo, _helper(topo, cores[j]), [cores[p] for p in _late(topo, cores, j)])))
 
     def blocks(n):
         return [(b, min(128, n - 128 * b)) for b in range((n + 127) // 128)]
 
-    runs = []
-    for p, e in enumerate(rackl):
-        if runs and runs[-1][1] + runs[-1][2] == e:
-            runs[-1][2] += 1
-        else:
-            runs.append([p, e, 1])
-
-    def scores(s):
-        need("pe", [arrive[s], RL])
+    def scores(s, before):
+        need("pe", [arrive[s], RL] + before)
         d = None
         for b, nb in blocks(nset[s]):
-            d = done("pe", g.tensor.matmul(sm[s][0:nb, 16 * b:16 * b + 16], xbuf[s][:, 128 * b:128 * b + nb],
+            c = 2 * s + b
+            d = done("pe", g.tensor.matmul(T.sm0[0:nb, 16 * c:16 * c + 16], xbuf[s][:, 128 * b:128 * b + nb],
                                            T.rts[:, :], True, True))
         return d
 
-    def softmax(s, d_sc):
-        n = nset[s]
-        bl = blocks(n)
+    def expo(s, d_sc):
+        bl = blocks(nset[s])
         need("ve", [d_sc])
         d = None
         for b, nb in bl:
             c = 2 * s + b
-            d = done("ve", g.vector.tensor_reduce(T.nmx[0:nb, c:c + 1], sm[s][0:nb, 16 * b:16 * b + 16],
+            d = done("ve", g.vector.tensor_reduce(T.nmx[0:nb, c:c + 1], T.sm0[0:nb, 16 * c:16 * c + 16],
                                                   AxisListType.X, AluOpType.max, negate=True))
         need("ac", [d, d_zs])
         for b, nb in bl:
             c = 2 * s + b
-            d = done("ac", g.scalar.activation(T.ex[0:nb, 16 * c:16 * c + 16], sm[s][0:nb, 16 * b:16 * b + 16],
+            d = done("ac", g.scalar.activation(T.ex[0:nb, 16 * c:16 * c + 16], T.sm0[0:nb, 16 * c:16 * c + 16],
                                                ActivationFunctionType.Exp, bias=T.nmx[0:nb, c:c + 1], scale=1.0,
                                                accum_out=T.zs[0:nb, c:c + 1]))
-        need("ve", [d])
-        d = done("ve", g.vector.reciprocal(T.rz[:, 2 * s:2 * s + len(bl)], T.zs[:, 2 * s:2 * s + len(bl)]))
-        need("ve", [d])
-        for b, nb in bl:
+        d_e = d
+        need("ve", [d_e])
+        d_r = done("ve", g.vector.reciprocal(T.rz[:, 2 * s:2 * s + len(bl)], T.zs[:, 2 * s:2 * s + len(bl)]))
+        return d_e, d_r
+
+    def diag(s, d_r):
+        need("ve", [d_r, CST])
+        d = None
+        for b, nb in blocks(nset[s]):
             c = 2 * s + b
-            for p, e, l in runs:
-                d = done("ve", g.vector.tensor_scalar(T.gm[0:nb, NE * c + p:NE * c + p + l],
-                                                      T.ex[0:nb, 16 * c + e:16 * c + e + l],
-                                                      T.rz[0:nb, c:c + 1], None, AluOpType.mult))
+            d = done("ve", g.vector.tensor_scalar(T.dg[0:nb, 128 * c:128 * c + nb], T.ident[0:nb, 0:nb],
+                                                  T.rz[0:nb, c:c + 1], None, AluOpType.mult))
         return d
 
-    def turn(s, d_g):
-        n = nset[s]
-        need("pe", [d_g, d_id])
-        d = None
-        for b, nb in blocks(n):
+    ring = {"n": 0, "free": [None] * len(zp)}
+
+    def run(s, groups, d_e, d_dg, accb):
+        first, final = groups[0][0], groups[-1][-1]
+        fin = {}
+        pend = []
+
+        def gather(G, b, nb, d_c):
             c = 2 * s + b
-            d = done("pe", g.tensor.matmul(sm[s][0:NE, 128 + 128 * b:128 + 128 * b + nb], T.gm[0:nb, NE * c:NE * c + NE],
-                                           T.ident[0:nb, 0:nb], True, True))
-        need("ac", [d])
-        return done("ac", g.scalar.activation(T.gts[0:NE, TK * s:TK * s + n], sm[s][0:NE, 128:128 + n],
-                                              ActivationFunctionType.Copy))
+            need("pe", [d_c, d_dg])
+            for j in G:
+                o = (c * NX + j) * 128
+                fin[b] = done("pe", g.tensor.matmul(accb[b][:, 0:nb], T.zg[0:nb, o:o + 128],
+                                                    T.dg[0:nb, 128 * c:128 * c + nb], j == first, j == final))
 
-    ring = {"n": 0, "free": [None, None, None, None]}
-    xgd = {}
+        for G in groups:
+            for b, nb in blocks(nset[s]):
+                if len(pend) == len(zp):
+                    gather(*pend.pop(0))
+                c = 2 * s + b
+                m = ring["n"]
+                k = m % len(zp)
+                ring["n"] += 1
+                deps = [wdep(j) for j in G] + [arrive[s]]
+                if ring["free"][k] is not None:
+                    deps.append(ring["free"][k])
+                need("pe", deps)
+                d = None
+                for u, j in enumerate(G):
+                    d = done("pe", g.tensor.matmul(zp[k][0:nb, 128 * u:128 * u + 128], xbuf[s][:, 128 * b:128 * b + nb],
+                                                   T.wall[:, j * 128:(j + 1) * 128], True, True))
+                eng = "ac" if m % 2 == 0 else "ve"
+                need(eng, [d, d_e])
+                for u, j in enumerate(G):
+                    o = (c * NX + j) * 128
+                    z = zp[k][0:nb, 128 * u:128 * u + 128]
+                    col = T.ex[0:nb, 16 * c + j:16 * c + j + 1]
+                    if eng == "ac":
+                        d = done("ac", g.scalar.activation(T.zg[0:nb, o:o + 128], z, ActivationFunctionType.Identity,
+                                                           bias=0.0, scale=col))
+                    else:
+                        d = done("ve", g.vector.tensor_scalar(T.zg[0:nb, o:o + 128], z, col, None, AluOpType.mult))
+                ring["free"][k] = d
+                pend.append((G, b, nb, d))
+        while pend:
+            gather(*pend.pop(0))
+        return fin
 
-    def gate(s, d_gt):
-        n = nset[s]
-        for j in order:
-            k = ring["n"] % 4
-            ring["n"] += 1
-            deps = [d_gt, d_sel]
-            if ring["free"][k] is not None:
-                deps.append(ring["free"][k])
-            need("pe", deps)
-            d = done("pe", g.tensor.matmul(gb[k][:, 0:n], T.sel[0:NE, j * 128:(j + 1) * 128],
-                                           T.gts[0:NE, TK * s:TK * s + n], True, True))
-            need("ve", [d, arrive[s]])
-            o = (s * NE + j) * TK
-            d = done("ve", g.vector.tensor_tensor(T.xg[:, o:o + n], xbuf[s][:, 0:n], gb[k][:, 0:n], AluOpType.mult))
-            ring["free"][k] = d
-            xgd[(s, j)] = d
-
-    def main(s, js):
-        n = nset[s]
-        d = None
-        for j in js:
-            need("pe", [wdep(j), xgd[(s, j)]])
-            o = (s * NE + j) * TK
-            d = done("pe", g.tensor.matmul(acc[s][:, 0:n], T.wall[:, j * 128:(j + 1) * 128], T.xg[:, o:o + n],
-                                           j == order[0], j == order[-1]))
-        return d
-
-    gate(0, turn(0, softmax(0, scores(0))))
-    d_sc = scores(1)
-    main(0, order[0:1])
-    gate(1, turn(1, softmax(1, d_sc)))
-    d_p = main(1, order)
-    d_o = main(0, order[1:])
-    n1 = nset[1]
-    need("ac", [d_p])
-    d_ev = done("ac", g.scalar.activation(T.pout[:, 0:n1], acc[1][:, 0:n1], ActivationFunctionType.Copy))
-    need("g", [d_ev])
+    e0, r0 = expo(0, scores(0, []))
+    e1, r1 = expo(1, scores(1, [e0]))
+    fp = run(1, [EP[0:3], EP[3:5], EP[5:6]], e1, diag(1, r1), [T.ap0, T.ap1])
+    ev = []
+    nb0 = min(128, n1)
+    need("ac", [fp[0]])
+    ev.append(done("ac", g.scalar.activation(T.pout[:, 0:nb0], T.ap0[:, 0:nb0], ActivationFunctionType.Copy)))
+    if 1 in fp:
+        need("ve", [fp[1]])
+        ev.append(done("ve", g.vector.tensor_copy(T.pout[:, 128:n1], T.ap1[:, 0:n1 - 128])))
+    need("g", ev)
     g.remote_dma(T.pin[:, 0:n1], T.pout[:, 0:n1], S.pa, S.sent, pid, rid, mx)
     sent += _bits(mx)
+    ao = [T.ao0, T.ao1]
+    fo = run(0, [EO[0:3], EO[3:6], EO[6:8], EO[8:9], EO[9:10]], e0, diag(0, r0), ao)
 
-    need("ve", [d_o, ("pa", _bits(topo.mask(pc, core)))])
-    d_y = done("ve", g.vector.tensor_tensor(T.yo[:, 0:n0], T.pin[:, 0:n0], acc[0][:, 0:n0], AluOpType.add))
+    d_y = None
+    for b, nb in blocks(n0):
+        need("ve", [fo[b], ("pa", _bits(topo.mask(pc, core)))])
+        d_y = done("ve", g.vector.tensor_tensor(T.yo[:, 128 * b:128 * b + nb], T.pin[:, 128 * b:128 * b + nb],
+                                                ao[b][:, 0:nb], AluOpType.add))
     need("sy", [d_y])
     g.sync.dma_start(T.y[:, 0:n0], T.yo[:, 0:n0]).then_inc(S.st, 16)
     g.sync.wait_ge(S.st, 16)

from concourse.bass import DstId, RemoteDMATransfer
from concourse.mybir import AluOpType, AxisListType, ActivationFunctionType

WORLD = 512
TK = 256
NX = 16
SCRATCH = {
    "xo": ("sbuf", [128, TK], "bfloat16"),
    "xp": ("sbuf", [128, TK], "bfloat16"),
    "rts": ("sbuf", [128, NX], "bfloat16"),
    "wall": ("sbuf", [128, NX * 128], "bfloat16"),
    "ramp": ("sbuf", [128, 128], "bfloat16"),
    "ident": ("sbuf", [128, 128], "bfloat16"),
    "nmx": ("sbuf", [128, 4], "float32"),
    "zs": ("sbuf", [128, 4], "float32"),
    "rz": ("sbuf", [128, 4], "float32"),
    "ex": ("sbuf", [128, 4 * NX], "float32"),
    "dg": ("sbuf", [128, 4 * 128], "bfloat16"),
    "zg": ("sbuf", [128, 4 * NX * 128], "bfloat16"),
    "pout": ("sbuf", [128, TK], "bfloat16"),
    "pin": ("sbuf", [128, TK], "bfloat16"),
    "yo": ("sbuf", [128, TK], "bfloat16"),
    "sm0": ("psum", [128, 512], "float32"),
    "ap0": ("psum", [128, 512], "float32"),
    "ap1": ("psum", [128, 512], "float32"),
    "ao0": ("psum", [128, 512], "float32"),
    "ao1": ("psum", [128, 512], "float32"),
    "zp0": ("psum", [128, 512], "float32"),
    "zp1": ("psum", [128, 512], "float32"),
    "zp2": ("psum", [128, 512], "float32"),
}
SEMAPHORES = ["xl", "rl", "wl", "st", "gi", "pe", "ve", "ac", "sent", "mp", "pa", "cst", "hw"] + ["w%d" % i for i in range(NX)]

_HC = {}


def _bits(m):
    return bin(m).count("1")


def _helper(topo, c):
    if c not in _HC:
        _HC[c] = [d for d in range(WORLD) if topo.host(d) == topo.host(c) and topo.chip(d) == topo.chip(c)
                  and topo.die(d) != topo.die(c)][0]
    return _HC[c]


def _plan(topo, cores, q):
    c = cores[q]
    R = range(len(cores))
    hl = [p for p in R if topo.host(cores[p]) == topo.host(c)]
    ml = [p for p in R if topo.host(cores[p]) != topo.host(c) and topo.same_plane(c, cores[p])]
    pa = [p for p in R if topo.rack(topo.host(cores[p])) != topo.rack(topo.host(c)) and topo.may_write(c, cores[p])
          and topo.chip(cores[p]) == topo.chip(c)][0]
    return hl, ml, pa, hl.index(q)


def _crit(topo, cores, q):
    hl, ml, pa, j = _plan(topo, cores, q)
    H = len(hl)
    return [ml[(j + k) % H] for k in range(H)] + [hl[(j + 1) % H]]


def _late(topo, cores, q):
    hl, ml, pa, j = _plan(topo, cores, q)
    H = len(hl)
    return [hl[(j + 2) % H], hl[(j + 3) % H], _plan(topo, cores, hl[(j - 1) % H])[2], _plan(topo, cores, hl[(j - 2) % H])[2]]


def _mask(topo, src, dsts):
    m = topo.mask(src, dsts[0])
    for d in dsts:
        m &= topo.mask(src, d)
    return m


def _chip_only(topo, src, on_chip, off_chip):
    return topo.mask(src, on_chip) & ~topo.mask(src, off_chip)


def _fan(g, T, topo, src, q, dsts, mask):
    slot = T.wall[:, q * 128:(q + 1) * 128]
    ids = []
    for d in dsts:
        r_, p_ = topo.addr(d, src)
        ids.append(DstId(rid=r_, pnc=p_))
    g.remote_dma_fused([RemoteDMATransfer(dst_ids=ids, dma_engine_mask=mask, remote_sem=T.sem["w%d" % q],
                                          srcs=[slot], dsts=[slot for _ in dsts])], local_sem=T.sem.sent)


def _helper_program(g, core, T, topo, q):
    cores = T.cores
    S = T.sem
    rc = cores[q]
    dsts = [cores[p] for p in _late(topo, cores, q)]
    mh = _mask(topo, core, dsts)
    g.iota(T.ramp[:, :], [[1, 128]], 0, -1, allow_small_or_imprecise_dtypes=True).then_inc(S.gi, 1)
    g.vector.wait_ge(S.gi, 1)
    g.vector.tensor_scalar(T.ident[:, :], T.ramp[:, :], 0.0, None, AluOpType.is_equal).then_inc(S.ve, 1)
    g.wait_ge(S.ve, 1)
    rid, pid = topo.addr(rc, core)
    g.remote_dma(T.ident[:, :], T.ident[:, :], S.cst, S.sent, pid, rid, mh)
    g.wait_ge(S.hw, _bits(_chip_only(topo, rc, core, dsts[0])))
    _fan(g, T, topo, core, q, dsts, mh)
    g.wait_ge(S.sent, 2 * _bits(mh))


def rank_program(g, core, T, topo):
    cores, wid = T.cores, T.tables["WID"]
    rank = T.rank_of(core)
    if rank is None:
        for q in range(len(cores)):
            if topo.host(cores[q]) == topo.host(core) and topo.chip(cores[q]) == topo.chip(core) \
                    and _helper(topo, cores[q]) == core:
                _helper_program(g, core, T, topo, q)
        return
    hl, ml, partner, i = _plan(topo, cores, rank)
    H = len(hl)
    phl, pml, _x, pi = _plan(topo, cores, partner)
    pc = cores[partner]
    hc = _helper(topo, core)
    EP = [rank] + [ml[(i - k) % H] for k in range(H)] + [hl[(i - 1) % H]]
    EO = EP + [hl[(i - 2) % H], hl[(i - 3) % H], phl[(pi + 1) % H], phl[(pi + 2) % H]]
    nset = [wid[rank], wid[partner]]
    xbuf = [T.xo, T.xp]
    zp = [T.zp0, T.zp1, T.zp2]
    S = T.sem
    Q = {"pe": g.tensor, "ve": g.vector, "ac": g.scalar, "g": g, "sy": g.sync}
    cnt = {"pe": 0, "ve": 0, "ac": 0}
    seen = {}

    def need(q, deps):
        for sem, val in deps:
            if seen.get((q, sem), 0) < val:
                Q[q].wait_ge(S[sem], val)
                seen[(q, sem)] = val

    def done(q, ins):
        ins.then_inc(S[q], 1)
        cnt[q] += 1
        return (q, cnt[q])

    n0, n1 = nset
    own = T.wall[:, rank * 128:(rank + 1) * 128]
    g.sync.dma_start(T.xo[:, 0:n0], T.x[:, 0:n0]).then_inc(S.xl, 16)
    g.scalar.dma_start(own, T.w[:, :]).then_inc(S.wl, 16)
    g.sync.dma_start(T.rts[:, :], T.rt[:, :]).then_inc(S.rl, 16)
    XL, RL, WL = ("xl", 16), ("rl", 16), ("wl", 16)
    d_zs = done("ve", g.vector.memset(T.zs[:, :], 1.0))

    mx = topo.mask(core, pc)
    rid, pid = topo.addr(pc, core)
    need("g", [XL])
    g.remote_dma(T.xp[:, 0:n0], T.xo[:, 0:n0], S.mp, S.sent, pid, rid, mx)
    sent = _bits(mx)
    cd = [cores[p] for p in _crit(topo, cores, rank)]
    mw = _mask(topo, core, cd)
    need("g", [WL])
    _fan(g, T, topo, core, rank, cd, mw)
    sent += _bits(mw)
    ld = [cores[p] for p in _late(topo, cores, rank)]
    mon = _chip_only(topo, core, hc, ld[0])
    hr, hp = topo.addr(hc, core)
    g.remote_dma(own, own, S.hw, S.sent, hp, hr, mon)
    sent += _bits(mon)
    MP = ("mp", _bits(topo.mask(pc, core)))
    arrive = [XL, MP]
    CST = ("cst", _bits(_mask(topo, hc, ld)))

    def wdep(j):
        if j == rank:
            return WL
        if rank in _crit(topo, cores, j):
            return ("w%d" % j, _bits(_mask(topo, cores[j], [cores[p] for p in _crit(topo, cores, j)])))
        return ("w%d" % j, _bits(_mask(topo, _helper(topo, cores[j]), [cores[p] for p in _late(topo, cores, j)])))

    def blocks(n):
        return [(b, min(128, n - 128 * b)) for b in range((n + 127) // 128)]

    def scores(s, before):
        need("pe", [arrive[s], RL] + before)
        d = None
        for b, nb in blocks(nset[s]):
            c = 2 * s + b
            d = done("pe", g.tensor.matmul(T.sm0[0:nb, 16 * c:16 * c + 16], xbuf[s][:, 128 * b:128 * b + nb],
                                           T.rts[:, :], True, True))
        return d

    def expo(s, d_sc):
        bl = blocks(nset[s])
        need("ve", [d_sc])
        d = None
        for b, nb in bl:
            c = 2 * s + b
            d = done("ve", g.vector.tensor_reduce(T.nmx[0:nb, c:c + 1], T.sm0[0:nb, 16 * c:16 * c + 16],
                                                  AxisListType.X, AluOpType.max, negate=True))
        need("ac", [d, d_zs])
        for b, nb in bl:
            c = 2 * s + b
            d = done("ac", g.scalar.activation(T.ex[0:nb, 16 * c:16 * c + 16], T.sm0[0:nb, 16 * c:16 * c + 16],
                                               ActivationFunctionType.Exp, bias=T.nmx[0:nb, c:c + 1], scale=1.0,
                                               accum_out=T.zs[0:nb, c:c + 1]))
        d_e = d
        need("ve", [d_e])
        d_r = done("ve", g.vector.reciprocal(T.rz[:, 2 * s:2 * s + len(bl)], T.zs[:, 2 * s:2 * s + len(bl)]))
        return d_e, d_r

    def diag(s, d_r):
        need("ve", [d_r, CST])
        d = None
        for b, nb in blocks(nset[s]):
            c = 2 * s + b
            d = done("ve", g.vector.tensor_scalar(T.dg[0:nb, 128 * c:128 * c + nb], T.ident[0:nb, 0:nb],
                                                  T.rz[0:nb, c:c + 1], None, AluOpType.mult))
        return d

    ring = {"n": 0, "free": [None] * len(zp)}

    def run(s, groups, d_e, d_dg, accb):
        first, final = groups[0][0], groups[-1][-1]
        fin = {}
        pend = []

        def gather(G, b, nb, d_c):
            c = 2 * s + b
            need("pe", [d_c, d_dg])
            for j in G:
                o = (c * NX + j) * 128
                fin[b] = done("pe", g.tensor.matmul(accb[b][:, 0:nb], T.zg[0:nb, o:o + 128],
                                                    T.dg[0:nb, 128 * c:128 * c + nb], j == first, j == final))

        for G in groups:
            for b, nb in blocks(nset[s]):
                if len(pend) == len(zp):
                    gather(*pend.pop(0))
                c = 2 * s + b
                m = ring["n"]
                k = m % len(zp)
                ring["n"] += 1
                deps = [wdep(j) for j in G] + [arrive[s]]
                if ring["free"][k] is not None:
                    deps.append(ring["free"][k])
                need("pe", deps)
                d = None
                for u, j in enumerate(G):
                    d = done("pe", g.tensor.matmul(zp[k][0:nb, 128 * u:128 * u + 128], xbuf[s][:, 128 * b:128 * b + nb],
                                                   T.wall[:, j * 128:(j + 1) * 128], True, True))
                eng = "ac" if m % 2 == 0 else "ve"
                need(eng, [d, d_e])
                for u, j in enumerate(G):
                    o = (c * NX + j) * 128
                    z = zp[k][0:nb, 128 * u:128 * u + 128]
                    col = T.ex[0:nb, 16 * c + j:16 * c + j + 1]
                    if eng == "ac":
                        d = done("ac", g.scalar.activation(T.zg[0:nb, o:o + 128], z, ActivationFunctionType.Identity,
                                                           bias=0.0, scale=col))
                    else:
                        d = done("ve", g.vector.tensor_scalar(T.zg[0:nb, o:o + 128], z, col, None, AluOpType.mult))
                ring["free"][k] = d
                pend.append((G, b, nb, d))
        while pend:
            gather(*pend.pop(0))
        return fin

    e0, r0 = expo(0, scores(0, []))
    e1, r1 = expo(1, scores(1, [e0]))
    fp = run(1, [EP[0:3], EP[3:5], EP[5:6]], e1, diag(1, r1), [T.ap0, T.ap1])
    ev = []
    nb0 = min(128, n1)
    need("ac", [fp[0]])
    ev.append(done("ac", g.scalar.activation(T.pout[:, 0:nb0], T.ap0[:, 0:nb0], ActivationFunctionType.Copy)))
    if 1 in fp:
        need("ve", [fp[1]])
        ev.append(done("ve", g.vector.tensor_copy(T.pout[:, 128:n1], T.ap1[:, 0:n1 - 128])))
    need("g", ev)
    g.remote_dma(T.pin[:, 0:n1], T.pout[:, 0:n1], S.pa, S.sent, pid, rid, mx)
    sent += _bits(mx)
    ao = [T.ao0, T.ao1]
    fo = run(0, [EO[0:3], EO[3:6], EO[6:8], EO[8:9], EO[9:10]], e0, diag(0, r0), ao)

    d_y = None
    for b, nb in blocks(n0):
        need("ve", [fo[b], ("pa", _bits(topo.mask(pc, core)))])
        d_y = done("ve", g.vector.tensor_tensor(T.yo[:, 128 * b:128 * b + nb], T.pin[:, 128 * b:128 * b + nb],
                                                ao[b][:, 0:nb], AluOpType.add))
    need("sy", [d_y])
    g.sync.dma_start(T.y[:, 0:n0], T.yo[:, 0:n0]).then_inc(S.st, 16)
    g.sync.wait_ge(S.st, 16)
    g.wait_ge(S.sent, sent)
